import numpy as np
import ml_dtypes


def mxq(x, axis, fmt="e4m3"):
    dtype, down = {"e4m3": (ml_dtypes.float8_e4m3fn, 7), "e5m2": (ml_dtypes.float8_e5m2, 14)}[fmt]
    v = np.moveaxis(np.asarray(x, np.float32).astype(ml_dtypes.bfloat16).astype(np.float64), axis, -1)
    blocks = v.reshape(v.shape[:-1] + (-1, 32))
    amax = np.abs(blocks).max(-1, keepdims=True)
    byte = np.maximum(np.where(amax > 0, np.frexp(amax)[1] - 1 + 127, 0) - down, 1)
    scale = np.exp2(byte - 127.0)
    codes = (blocks / scale).astype(np.float32).astype(dtype).astype(np.float64)
    return np.moveaxis((codes * scale).reshape(v.shape), -1, axis)


WIDE = False


def mx_kscale(k):
    if not WIDE:
        return np.ones(k)
    levels = np.array([10, -10, 5, -5, 0])
    if k % 512:
        return np.exp2(np.random.permutation(np.resize(levels, k // 32))).repeat(32)
    a = np.empty((k // 512, 16))
    for p in range(k // 512):
        a[p, :8] = np.random.permutation(np.resize(levels, 8))
        for g in range(8):
            far = levels[np.abs(levels - a[p, g]) >= 10]
            a[p, g + 8] = far[np.random.randint(len(far))]
    return np.exp2(a.ravel()).repeat(32)


BF16 = ml_dtypes.bfloat16


def bf(x):
    return np.asarray(x, np.float32).astype(BF16)


def f64(x):
    return np.asarray(x).astype(np.float64)


E2M1 = np.array([0.0, 0.5, 1.0, 1.5, 2.0, 3.0, 4.0, 6.0, -0.0, -0.5, -1.0, -1.5, -2.0, -3.0, -4.0, -6.0])


def pack_weight(w, fmt):
    k, n = w.shape
    w = f64(bf(w)).reshape(k // 32, 32, n)
    amax = np.abs(w).max(1)
    if fmt == "e4m3":
        byte = np.frexp(amax)[1] - 1 + 127 - 7
    else:
        mant, ex = np.frexp(amax / 6.0)
        byte = np.where(mant > 0.5, ex, ex - 1) + 127
    byte = np.clip(np.where(amax > 0, byte, 1), 1, 254)
    scaled = (w * np.exp2(127.0 - byte)[:, None, :]).reshape(k, n).astype(np.float32)
    by_word = np.ascontiguousarray(scaled.reshape(k // 512, 128, 4, n).transpose(0, 1, 3, 2))
    if fmt == "e4m3":
        words = by_word.astype(ml_dtypes.float8_e4m3fn).view(np.uint8)
    else:
        c = by_word.astype(ml_dtypes.float4_e2m1fn).view(np.uint8) & 0xF
        words = c[..., 0::2] | (c[..., 1::2] << 4)
    return np.ascontiguousarray(words), np.ascontiguousarray(byte.astype(np.uint8).reshape(k // 512, 16, n))


def unpack_weight(words, scales, fmt):
    g, p, n, _ = words.shape
    if fmt == "e4m3":
        vals = np.ascontiguousarray(words).view(ml_dtypes.float8_e4m3fn).astype(np.float64)
    else:
        nib = np.empty((g, p, n, 4), np.uint8)
        nib[..., 0::2] = words & 0xF
        nib[..., 1::2] = words >> 4
        vals = E2M1[nib]
    vals = vals * np.repeat(np.exp2(scales.astype(np.float64) - 127.0), 8, axis=1)[..., None]
    return vals.transpose(0, 1, 3, 2).reshape(g * 512, n)
def pack4(w):
    words, scales = pack_weight(w, "e2m1")
    return words.reshape(words.shape[0], 128, -1), scales


def unpack4(words, scales):
    return unpack_weight(words.reshape(words.shape[0], 128, -1, 2), scales, "e2m1")


def planes(Y):
    n, m = Y.shape
    b = f64(bf(Y)).reshape(n // 32, 32, m)
    amax = np.abs(b).max(1)
    byte = np.clip(np.where(amax > 0, np.frexp(amax)[1] - 1 + 127 - 7, 1), 1, 254)
    codes = (b * np.exp2(127.0 - byte)[:, None, :]).reshape(n, m).astype(np.float32).astype(ml_dtypes.float8_e4m3fn).view(np.uint8)
    words = codes.reshape(n // 512, 128, 4, m).transpose(0, 1, 3, 2)
    return np.ascontiguousarray(words), np.ascontiguousarray(byte.astype(np.uint8).reshape(n // 512, 16, m))


L, R, F = 4, 1024, 512
EPS_BAR, EPS_GAP, FILL = 9.0, 1.0, 0.25


def permittivity_toeplitz():
    half = np.where(np.random.rand(L, F + 1) < FILL, EPS_BAR, EPS_GAP)
    profile = np.concatenate([half, half[:, F - 1:0:-1]], axis=1)
    coef = np.fft.fft(profile, axis=1).real / (2 * F)
    n = np.arange(F)
    return coef[:, np.abs(n[:, None] - n[None, :])]


def setup_inputs():
    s = mx_kscale(F)
    E = permittivity_toeplitz()
    Einv = np.linalg.inv(E)
    kx0 = np.random.uniform(0.1, 0.9)
    kx = kx0 + (np.arange(F) - F / 2) * (4.0 / F)
    einv_words, einv_scales = pack4((Einv / (s * s)[:, None]).reshape(L * F, F))
    eps_words, eps_scales = pack4((E / s[:, None]).reshape(L * F, F))
    return {
        "u": bf(0.5 * np.random.randn(L, R, F) * s),
        "kx": bf(kx * s),
        "einv_words": einv_words, "einv_scales": einv_scales,
        "eps_words": eps_words, "eps_scales": eps_scales,
        "source": bf(np.random.randn(L, R, F)),
        "hscale": bf(np.exp(0.8 * np.random.randn(L, F))),
    }


def reference(u, kx, einv_words, einv_scales, eps_words, eps_scales, source, hscale):
    u, kx, source, hscale = f64(u), f64(kx), f64(source), f64(hscale)
    A = unpack4(einv_words, einv_scales).reshape(L, F, F)
    E = unpack4(eps_words, eps_scales).reshape(L, F, F)
    h = mxq(u * kx, 2) @ A
    z = h * kx - u
    v = mxq(z, 2) @ E
    y = (v + source) * hscale[:, None, :]
    Y = y.reshape(L * R, F).T
    words, scales = planes(Y)
    return y, words, scales

@@ -1,0 +1,307 @@
+from contextlib import ExitStack
+
+import concourse.mybir as mybir
+from concourse.masks import make_identity
+
+L, R, F = 4, 1024, 512
+FLOPS = 2 * 2 * L * R * F * F
+
+F32 = mybir.dt.float32
+BF16 = mybir.dt.bfloat16
+I32 = mybir.dt.int32
+U32 = mybir.dt.uint32
+U8 = mybir.dt.uint8
+FP8X4 = mybir.dt.float8_e4m3fn_x4
+FP4X4 = mybir.dt.float4_e2m1fn_x4
+ALU = mybir.AluOpType
+ACT = mybir.ActivationFunctionType
+
+P = 128
+PACK = 4
+T = 256
+J = T // P
+CHUNKS = L * R // T
+PER_LAYER = R // T
+LATE = 64
+ON_GPSIMD = CHUNKS - 2
+
+
+def tile_layered_coupled_wave_operator_k7_kernel(
+    tc, u, kx, einv_words, einv_scales, eps_words, eps_scales, source, hscale, out_0, out_1, out_2
+):
+    nc = tc.nc
+    u_rows = u.rearrange("l r f -> (l r) f")
+    src_rows = source.rearrange("l r f -> (l r) f")
+    y_rows = out_0.rearrange("l r f -> (l r) f")
+    words_out = out_1[0].rearrange("p m t -> p (m t)").bitcast(I32)
+    scales_out = out_2[0].bitcast(I32)
+
+    def chunk_rows(rows, c):
+        return rows[c * T : (c + 1) * T, :].rearrange("(p j) f -> p j f", j=J)
+
+    with ExitStack() as ctx:
+        keep = ctx.enter_context(tc.tile_pool(name="keep", bufs=1))
+        work = ctx.enter_context(tc.tile_pool(name="work", bufs=3))
+        psum = ctx.enter_context(tc.psum_pool(name="psum", bufs=1))
+        ctx.enter_context(tc.manual_schedule())
+
+        ident = keep.tile([P, P], F32, name="ident")
+        kx_bf = keep.tile([P, PACK], BF16, name="kx_bf")
+        kx_f32 = keep.tile([P, PACK], F32, name="kx_f32")
+        a_raw = keep.tile([P, L, 2 * F], U8, name="a_raw", align_bytes=64)
+        a_raw_scales = keep.tile([P, L, F], U8, name="a_raw_scales", align_bytes=64)
+        a_words = keep.tile([P, L, 2 * F], U8, name="a_words", align_bytes=64)
+        a_scales = keep.tile([P, L, F], U8, name="a_scales", align_bytes=64)
+        e_words = keep.tile([P, L, 2 * F], U8, name="e_words", align_bytes=64)
+        e_scales = keep.tile([P, L, F], U8, name="e_scales", align_bytes=64)
+        h_rep = keep.tile([P, L, F], BF16, name="h_rep")
+        y_codes = keep.tile([P, L * R], U32, name="y_codes", align_bytes=64)
+        y_scales = keep.tile([P, L * R], U8, name="y_scales", align_bytes=64)
+        u_sb = [keep.tile([P, J, F], BF16, name="u_%d" % c) for c in range(CHUNKS)]
+        src_sb = [keep.tile([P, J, F], BF16, name="src_%d" % c) for c in range(CHUNKS)]
+
+        def load_words(dst, words, l0, l1):
+            nc.sync.dma_start(
+                out=dst[:, l0:l1, :].bitcast(I32), in_=words[l0:l1].rearrange("l p n -> p l n").bitcast(I32)
+            )
+
+        def load_scales(dst, scales):
+            for q in range(4):
+                nc.scalar.dma_start(
+                    out=dst[32 * q : 32 * q + 4, :, :].bitcast(I32),
+                    in_=scales[:, 4 * q : 4 * q + 4, :].rearrange("l r n -> r l n").bitcast(I32),
+                )
+
+        def load_h(l):
+            nc.sync.dma_start(out=h_rep[:, l, :], in_=hscale[l].partition_broadcast(P))
+
+        nc.vector.memset(a_raw_scales[:].bitcast(I32), 0)
+        nc.vector.memset(e_scales[:].bitcast(I32), 0)
+        make_identity(nc, ident[:])
+        nc.sync.dma_start(out=u_sb[0][:], in_=chunk_rows(u_rows, 0))
+        nc.scalar.dma_start(out=kx_bf[:], in_=kx.rearrange("(p t) -> p t", t=PACK))
+        load_words(a_raw, einv_words, 0, 1)
+        load_scales(a_raw_scales, einv_scales)
+        nc.sync.dma_start(out=u_sb[1][:], in_=chunk_rows(u_rows, 1))
+        load_words(a_raw, einv_words, 1, L)
+        load_words(e_words, eps_words, 0, 1)
+        load_scales(e_scales, eps_scales)
+        nc.scalar.activation(out=kx_f32[:], in_=kx_bf[:], func=ACT.Copy)
+        for c in range(CHUNKS):
+            if c + 2 < CHUNKS:
+                nc.sync.dma_start(out=u_sb[c + 2][:], in_=chunk_rows(u_rows, c + 2))
+            nc.sync.dma_start(out=src_sb[c][:], in_=chunk_rows(src_rows, c))
+            if c % PER_LAYER == 0:
+                load_h(c // PER_LAYER)
+            if c == 1:
+                load_words(e_words, eps_words, 1, L)
+
+        uT, x_bf, xq, xs, hp, hk, z_bf, zq, zs, vp, w, y, y_bf, yT, y_il = ({} for n in range(15))
+
+        def permute_words(l):
+            nc.vector.tensor_copy(
+                out=a_words[:, l, :].rearrange("p (t m b) -> p t m b", t=PACK, b=2),
+                in_=a_raw[:, l, :].rearrange("p (m t b) -> p t m b", t=PACK, b=2),
+            )
+
+        def permute_scales(l):
+            nc.vector.tensor_copy(
+                out=a_scales[:, l, :].rearrange("p (t m) -> p t m", t=PACK),
+                in_=a_raw_scales[:, l, :].rearrange("p (m t) -> p t m", t=PACK),
+            )
+
+        def transpose_words(dst, rows):
+            for j in range(J):
+                pairs = rows[:, j, :].bitcast(F32)
+                for s in range(2):
+                    nc.tensor.transpose(dst[:, s, j * P : (j + 1) * P], pairs[:, s : F // 2 : 2], ident[:])
+
+        def transpose_u(c):
+            uT[c] = psum.tile([P, 2, T], F32, name="uT", bufs=3)
+            transpose_words(uT[c], u_sb[c])
+
+        def u_view(c):
+            return uT[c][:].bitcast(BF16).rearrange("p s (n e) -> p n s e", e=2)
+
+        def make_x(c):
+            x_bf[c] = work.tile([P, T * PACK], BF16, name="x_bf", align_bytes=64)
+            nc.vector.tensor_tensor(
+                out=x_bf[c][:].rearrange("p (n s e) -> p n s e", s=2, e=2),
+                in0=u_view(c),
+                in1=kx_bf[:].rearrange("p (s e) -> p s e", e=2).unsqueeze(1).to_broadcast([P, T, 2, 2]),
+                op=ALU.mult,
+            )
+
+        def quantize_x(c):
+            xq[c] = work.tile([P, T], U32, name="xq", align_bytes=64)
+            xs[c] = work.tile([P, T], U8, name="xs", align_bytes=64)
+            nc.vector.quantize_mx(out=xq[c][:].bitcast(FP8X4), scales=xs[c][:], in_=x_bf[c][:])
+
+        def matmul_h(c, s):
+            l = c // PER_LAYER
+            hp[c, s] = psum.tile([P, 2, T], F32, name="hp%d" % s)
+            for e in range(2):
+                t = 2 * s + e
+                nc.tensor.matmul_mx(
+                    out=hp[c, s][:, e, :],
+                    lhsT=a_words[:, l, 2 * P * t : 2 * P * (t + 1)].bitcast(FP4X4),
+                    lhsT_scale=a_scales[:, l, P * t : P * (t + 1)],
+                    rhs=xq[c][:].bitcast(FP8X4),
+                    rhs_scale=xs[c][:],
+                    start=True,
+                    stop=True,
+                )
+
+        def scale_h(c):
+            hk[c] = work.tile([P, PACK, T], F32, name="hk")
+            for t in range(PACK):
+                nc.scalar.activation(
+                    out=hk[c][:, t, :], in_=hp[c, t // 2][:, t % 2, :], func=ACT.Copy, scale=kx_f32[:, t : t + 1]
+                )
+
+        def make_z(c):
+            z_bf[c] = work.tile([P, T * PACK], BF16, name="z_bf", align_bytes=64)
+            nc.vector.tensor_tensor(
+                out=z_bf[c][:].rearrange("p (n s e) -> p n s e", s=2, e=2),
+                in0=hk[c][:].rearrange("p (s e) n -> p n s e", e=2),
+                in1=u_view(c),
+                op=ALU.subtract,
+            )
+
+        def quantize_z(c):
+            zq[c] = work.tile([P, T], U32, name="zq", align_bytes=64)
+            zs[c] = work.tile([P, T], U8, name="zs", align_bytes=64)
+            nc.vector.quantize_mx(out=zq[c][:].bitcast(FP8X4), scales=zs[c][:], in_=z_bf[c][:])
+
+        def matmul_v(c, j):
+            l = c // PER_LAYER
+            vp[c, j] = psum.tile([P, F], F32, name="vp%d" % j)
+            nc.tensor.matmul_mx(
+                out=vp[c, j][:],
+                lhsT=zq[c][:, j * P : (j + 1) * P].bitcast(FP8X4),
+                lhsT_scale=zs[c][:, j * P : (j + 1) * P],
+                rhs=e_words[:, l, :].bitcast(FP4X4),
+                rhs_scale=e_scales[:, l, :],
+                start=True,
+                stop=True,
+            )
+
+        def add_source(c, j, f0, f1):
+            nc.vector.tensor_tensor(
+                out=w[c][:, j, f0:f1], in0=vp[c, j][:, f0:f1], in1=src_sb[c][:, j, f0:f1], op=ALU.add
+            )
+
+        def add_source_early(c):
+            w[c] = work.tile([P, J, F], F32, name="w")
+            add_source(c, 0, 0, F)
+            add_source(c, 1, 0, F - LATE if c < ON_GPSIMD else F)
+
+        def make_y(c):
+            l = c // PER_LAYER
+            y[c] = work.tile([P, J, F], F32, name="y", bufs=4)
+            nc.gpsimd.tensor_tensor(
+                out=y[c][:], in0=w[c][:], in1=h_rep[:, l, :].unsqueeze(1).to_broadcast([P, J, F]), op=ALU.mult
+            )
+            nc.sync.dma_start(out=chunk_rows(y_rows, c), in_=y[c][:])
+
+        def round_y(c):
+            y_bf[c] = work.tile([P, J, F], BF16, name="y_bf")
+            nc.scalar.copy(out=y_bf[c][:], in_=y[c][:])
+
+        def transpose_y(c):
+            yT[c] = psum.tile([P, 2, T], F32, name="yT")
+            transpose_words(yT[c], y_bf[c])
+            y_il[c] = work.tile([P, T * PACK], BF16, name="y_il", bufs=4, align_bytes=64)
+            nc.scalar.copy(
+                out=y_il[c][:].bitcast(F32).rearrange("p (n j s) -> p n j s", j=J, s=2),
+                in_=yT[c][:].rearrange("p s (j n) -> p n j s", j=J),
+            )
+
+        def quantize_y(c):
+            cols = slice(c * T, (c + 1) * T)
+            nc.vector.quantize_mx(out=y_codes[:, cols].bitcast(FP8X4), scales=y_scales[:, cols], in_=y_il[c][:])
+            nc.sync.dma_start(out=words_out[:, cols], in_=y_codes[:, cols].bitcast(I32))
+            if c in (11, 15):
+                c0 = 0 if c == 11 else 12
+                for q in range(4):
+                    nc.sync.dma_start(
+                        out=scales_out[4 * q : 4 * q + 4, c0 * T // 4 : (c + 1) * T // 4],
+                        in_=y_scales[32 * q : 32 * q + 4, c0 * T : (c + 1) * T].bitcast(I32),
+                    )
+
+        def finish_half(c, j):
+            l = c // PER_LAYER
+            nc.vector.tensor_tensor(out=y[c][:, j, :], in0=w[c][:, j, :], in1=h_rep[:, l, :], op=ALU.mult)
+            nc.sync.dma_start(out=chunk_rows(y_rows, c)[:, j, :], in_=y[c][:, j, :])
+
+        def live(c):
+            return 0 <= c < CHUNKS
+
+        transpose_u(0)
+        transpose_u(1)
+        permute_words(0)
+        make_x(0)
+        permute_scales(0)
+        for i in range(CHUNKS):
+            if live(i):
+                quantize_x(i)
+            if live(i - 1):
+                quantize_z(i - 1)
+            if live(i - 4):
+                quantize_y(i - 4)
+            if 0 <= i - 2 < ON_GPSIMD:
+                add_source(i - 2, 1, F - LATE, F)
+                make_y(i - 2)
+            if live(i - 3):
+                round_y(i - 3)
+            for s in range(2):
+                if live(i):
+                    matmul_h(i, s)
+                if live(i - 1):
+                    matmul_v(i - 1, s)
+            if live(i):
+                scale_h(i)
+            if live(i + 1):
+                make_x(i + 1)
+            if i == 0:
+                permute_words(1)
+                permute_scales(1)
+                permute_words(2)
+            if i == 1:
+                permute_scales(2)
+                permute_words(3)
+                permute_scales(3)
+            if live(i - 1):
+                add_source_early(i - 1)
+            if live(i):
+                make_z(i)
+            if live(i + 2):
+                transpose_u(i + 2)
+            if live(i - 3):
+                transpose_y(i - 3)
+
+        a, b = CHUNKS - 2, CHUNKS - 1
+        round_y(a - 1)
+        for c in (a, b):
+            y[c] = work.tile([P, J, F], F32, name="y", bufs=4)
+            y_bf[c] = work.tile([P, J, F], BF16, name="y_bf")
+        w[b] = work.tile([P, J, F], F32, name="w")
+        quantize_z(b)
+        matmul_v(b, 0)
+        matmul_v(b, 1)
+        for j in range(J):
+            finish_half(a, j)
+            nc.scalar.copy(out=y_bf[a][:, j, :], in_=y[a][:, j, :])
+        transpose_y(a - 1)
+        transpose_y(a)
+        for j in range(J):
+            add_source(b, j, 0, F)
+        for j in range(J):
+            finish_half(b, j)
+        for j in range(J):
+            nc.vector.tensor_copy(out=y_bf[b][:, j, :], in_=y[b][:, j, :])
+        quantize_y(a - 2)
+        quantize_y(a - 1)
+        transpose_y(b)
+        quantize_y(a)
+        quantize_y(b)

@@ -174,10 +174,13 @@ def tile_layered_coupled_wave_operator_k7_kernel(
             nc.vector.quantize_mx(out=zq[c][:].bitcast(FP8X4), scales=zs[c][:], in_=z_bf[c][:])
 
         def matmul_v(c, j):
-            l = c // PER_LAYER
             vp[c, j] = psum.tile([P, F], F32, name="vp%d" % j)
+            product_v(vp[c, j][:], c, j)
+
+        def product_v(dst, c, j):
+            l = c // PER_LAYER
             nc.tensor.matmul_mx(
-                out=vp[c, j][:],
+                out=dst,
                 lhsT=zq[c][:, j * P : (j + 1) * P].bitcast(FP8X4),
                 lhsT_scale=zs[c][:, j * P : (j + 1) * P],
                 rhs=e_words[:, l, :].bitcast(FP4X4),
@@ -204,13 +207,25 @@ def tile_layered_coupled_wave_operator_k7_kernel(
             )
             nc.sync.dma_start(out=chunk_rows(y_rows, c), in_=y[c][:])
 
+        def pair_order(rows):
+            return rows.rearrange("p j (s m e) -> p j s m e", s=2, e=2)
+
+        def pairs_of(rows):
+            return rows.rearrange("p j (m s e) -> p j s m e", s=2, e=2)
+
         def round_y(c):
             y_bf[c] = work.tile([P, J, F], BF16, name="y_bf")
-            nc.scalar.copy(out=y_bf[c][:], in_=y[c][:])
+            nc.scalar.copy(out=pair_order(y_bf[c][:]), in_=pairs_of(y[c][:]))
 
-        def transpose_y(c):
+        def transpose_y(c, warm=None):
             yT[c] = psum.tile([P, 2, T], F32, name="yT")
-            transpose_words(yT[c], y_bf[c])
+            if warm is not None:
+                for j in range(J):
+                    product_v(yT[c][:].rearrange("p s n -> p (s n)"), warm, j)
+            for j in range(J):
+                pairs = y_bf[c][:, j, :].bitcast(F32)
+                for s in range(2):
+                    nc.tensor.transpose(yT[c][:, s, j * P : (j + 1) * P], pairs[:, s * P : (s + 1) * P], ident[:])
             y_il[c] = work.tile([P, T * PACK], BF16, name="y_il", bufs=4, align_bytes=64)
             nc.scalar.copy(
                 out=y_il[c][:].bitcast(F32).rearrange("p (n j s) -> p n j s", j=J, s=2),
@@ -252,8 +267,6 @@ def tile_layered_coupled_wave_operator_k7_kernel(
             if 0 <= i - 2 < ON_GPSIMD:
                 add_source(i - 2, 1, F - LATE, F)
                 make_y(i - 2)
-            if live(i - 3):
-                round_y(i - 3)
             for s in range(2):
                 if live(i):
                     matmul_h(i, s)
@@ -261,6 +274,8 @@ def tile_layered_coupled_wave_operator_k7_kernel(
                     matmul_v(i - 1, s)
             if live(i):
                 scale_h(i)
+            if live(i - 3):
+                round_y(i - 3)
             if live(i + 1):
                 make_x(i + 1)
             if i == 0:
@@ -278,7 +293,7 @@ def tile_layered_coupled_wave_operator_k7_kernel(
             if live(i + 2):
                 transpose_u(i + 2)
             if live(i - 3):
-                transpose_y(i - 3)
+                transpose_y(i - 3, i - 1)
 
         a, b = CHUNKS - 2, CHUNKS - 1
         round_y(a - 1)
@@ -291,7 +306,7 @@ def tile_layered_coupled_wave_operator_k7_kernel(
         matmul_v(b, 1)
         for j in range(J):
             finish_half(a, j)
-            nc.scalar.copy(out=y_bf[a][:, j, :], in_=y[a][:, j, :])
+            nc.scalar.copy(out=pair_order(y_bf[a][:, j : j + 1, :]), in_=pairs_of(y[a][:, j : j + 1, :]))
         transpose_y(a - 1)
         transpose_y(a)
         for j in range(J):
@@ -299,7 +314,7 @@ def tile_layered_coupled_wave_operator_k7_kernel(
         for j in range(J):
             finish_half(b, j)
         for j in range(J):
-            nc.vector.tensor_copy(out=y_bf[b][:, j, :], in_=y[b][:, j, :])
+            nc.vector.tensor_copy(out=pair_order(y_bf[b][:, j : j + 1, :]), in_=pairs_of(y[b][:, j : j + 1, :]))
         quantize_y(a - 2)
         quantize_y(a - 1)
         transpose_y(b)

@@ -127,8 +127,8 @@ def tile_layered_coupled_wave_operator_k7_kernel(
             x_bf[c] = work.tile([P, T * PACK], BF16, name="x_bf", align_bytes=64)
             nc.vector.tensor_tensor(
                 out=x_bf[c][:].rearrange("p (n s e) -> p n s e", s=2, e=2),
-                in0=u_view(c),
-                in1=kx_bf[:].rearrange("p (s e) -> p s e", e=2).unsqueeze(1).to_broadcast([P, T, 2, 2]),
+                in0=kx_bf[:].rearrange("p (s e) -> p s e", e=2).unsqueeze(1).to_broadcast([P, T, 2, 2]),
+                in1=u_view(c),
                 op=ALU.mult,
             )
 
@@ -191,7 +191,7 @@ def tile_layered_coupled_wave_operator_k7_kernel(
 
         def add_source(c, j, f0, f1):
             nc.vector.tensor_tensor(
-                out=w[c][:, j, f0:f1], in0=vp[c, j][:, f0:f1], in1=src_sb[c][:, j, f0:f1], op=ALU.add
+                out=w[c][:, j, f0:f1], in0=src_sb[c][:, j, f0:f1], in1=vp[c, j][:, f0:f1], op=ALU.add
             )
 
         def add_source_early(c):
@@ -217,11 +217,8 @@ def tile_layered_coupled_wave_operator_k7_kernel(
             y_bf[c] = work.tile([P, J, F], BF16, name="y_bf")
             nc.scalar.copy(out=pair_order(y_bf[c][:]), in_=pairs_of(y[c][:]))
 
-        def transpose_y(c, warm=None):
+        def transpose_y(c):
             yT[c] = psum.tile([P, 2, T], F32, name="yT")
-            if warm is not None:
-                for j in range(J):
-                    product_v(yT[c][:].rearrange("p s n -> p (s n)"), warm, j)
             for j in range(J):
                 pairs = y_bf[c][:, j, :].bitcast(F32)
                 for s in range(2):
@@ -257,43 +254,44 @@ def tile_layered_coupled_wave_operator_k7_kernel(
         permute_words(0)
         make_x(0)
         permute_scales(0)
-        for i in range(CHUNKS):
-            if live(i):
-                quantize_x(i)
+        for i in range(-1, CHUNKS):
             if live(i - 1):
                 quantize_z(i - 1)
+            if live(i + 1):
+                quantize_x(i + 1)
             if live(i - 4):
                 quantize_y(i - 4)
             if 0 <= i - 2 < ON_GPSIMD:
                 add_source(i - 2, 1, F - LATE, F)
                 make_y(i - 2)
-            for s in range(2):
-                if live(i):
-                    matmul_h(i, s)
-                if live(i - 1):
-                    matmul_v(i - 1, s)
-            if live(i):
-                scale_h(i)
             if live(i - 3):
                 round_y(i - 3)
+            if live(i - 1):
+                matmul_v(i - 1, 0)
             if live(i + 1):
-                make_x(i + 1)
-            if i == 0:
+                matmul_h(i + 1, 0)
+                matmul_h(i + 1, 1)
+                scale_h(i + 1)
+            if live(i - 1):
+                matmul_v(i - 1, 1)
+            if live(i + 2):
+                make_x(i + 2)
+            if i == -1:
                 permute_words(1)
                 permute_scales(1)
                 permute_words(2)
-            if i == 1:
+            if live(i):
+                make_z(i)
+            if i == 0:
                 permute_scales(2)
                 permute_words(3)
                 permute_scales(3)
             if live(i - 1):
                 add_source_early(i - 1)
-            if live(i):
-                make_z(i)
-            if live(i + 2):
-                transpose_u(i + 2)
             if live(i - 3):
-                transpose_y(i - 3, i - 1)
+                transpose_y(i - 3)
+            if live(i + 3):
+                transpose_u(i + 3)
 
         a, b = CHUNKS - 2, CHUNKS - 1
         round_y(a - 1)

@@ -24,6 +24,7 @@ CHUNKS = L * R // T
 PER_LAYER = R // T
 LATE = 64
 ON_GPSIMD = CHUNKS - 2
+X_ON_SCALAR = [c for c in range(CHUNKS - 2) if c % 5 in (2, 4)]
 
 
 def tile_layered_coupled_wave_operator_k7_kernel(
@@ -97,6 +98,7 @@ def tile_layered_coupled_wave_operator_k7_kernel(
                 load_words(e_words, eps_words, 1, L)
 
         uT, x_bf, xq, xs, hp, hk, z_bf, zq, zs, vp, w, y, y_bf, yT, y_il = ({} for n in range(15))
+        x_rows = {}
 
         def permute_words(l):
             nc.vector.tensor_copy(
@@ -130,6 +132,22 @@ def tile_layered_coupled_wave_operator_k7_kernel(
                 in0=kx_bf[:].rearrange("p (s e) -> p s e", e=2).unsqueeze(1).to_broadcast([P, T, 2, 2]),
                 in1=u_view(c),
                 op=ALU.mult,
+            )
+
+        def scale_u(c):
+            x_rows[c] = work.tile([P, PACK, T], BF16, name="x_rows", bufs=2)
+            for t in range(PACK):
+                nc.scalar.activation(
+                    out=x_rows[c][:, t, :],
+                    in_=uT[c][:, t // 2, :].bitcast(BF16)[:, t % 2 : 2 * T : 2],
+                    func=ACT.Copy,
+                    scale=kx_f32[:, t : t + 1],
+                )
+
+        def interleave_x(c):
+            x_bf[c] = work.tile([P, T * PACK], BF16, name="x_bf", align_bytes=64)
+            nc.scalar.copy(
+                out=x_bf[c][:].rearrange("p (n t) -> p n t", t=PACK), in_=x_rows[c][:].rearrange("p t n -> p n t")
             )
 
         def quantize_x(c):
@@ -223,7 +241,7 @@ def tile_layered_coupled_wave_operator_k7_kernel(
                 pairs = y_bf[c][:, j, :].bitcast(F32)
                 for s in range(2):
                     nc.tensor.transpose(yT[c][:, s, j * P : (j + 1) * P], pairs[:, s * P : (s + 1) * P], ident[:])
-            y_il[c] = work.tile([P, T * PACK], BF16, name="y_il", bufs=4, align_bytes=64)
+            y_il[c] = work.tile([P, T * PACK], BF16, name="y_il", bufs=5, align_bytes=64)
             nc.scalar.copy(
                 out=y_il[c][:].bitcast(F32).rearrange("p (n j s) -> p n j s", j=J, s=2),
                 in_=yT[c][:].rearrange("p s (j n) -> p n j s", j=J),
@@ -259,13 +277,19 @@ def tile_layered_coupled_wave_operator_k7_kernel(
                 quantize_z(i - 1)
             if live(i + 1):
                 quantize_x(i + 1)
-            if live(i - 4):
-                quantize_y(i - 4)
+            x_on_vector = live(i + 2) and i + 2 not in X_ON_SCALAR
+            if live(i - 5) and x_on_vector:
+                quantize_y(i - 5)
             if 0 <= i - 2 < ON_GPSIMD:
                 add_source(i - 2, 1, F - LATE, F)
+            if live(i - 5) and not x_on_vector:
+                quantize_y(i - 5)
+            if 0 <= i - 2 < ON_GPSIMD:
                 make_y(i - 2)
             if live(i - 3):
                 round_y(i - 3)
+            if i + 2 in X_ON_SCALAR:
+                interleave_x(i + 2)
             if live(i - 1):
                 matmul_v(i - 1, 0)
             if live(i + 1):
@@ -274,7 +298,7 @@ def tile_layered_coupled_wave_operator_k7_kernel(
                 scale_h(i + 1)
             if live(i - 1):
                 matmul_v(i - 1, 1)
-            if live(i + 2):
+            if x_on_vector:
                 make_x(i + 2)
             if i == -1:
                 permute_words(1)
@@ -292,6 +316,8 @@ def tile_layered_coupled_wave_operator_k7_kernel(
                 transpose_y(i - 3)
             if live(i + 3):
                 transpose_u(i + 3)
+            if i + 3 in X_ON_SCALAR:
+                scale_u(i + 3)
 
         a, b = CHUNKS - 2, CHUNKS - 1
         round_y(a - 1)
@@ -300,6 +326,7 @@ def tile_layered_coupled_wave_operator_k7_kernel(
             y_bf[c] = work.tile([P, J, F], BF16, name="y_bf")
         w[b] = work.tile([P, J, F], F32, name="w")
         quantize_z(b)
+        quantize_y(a - 3)
         matmul_v(b, 0)
         matmul_v(b, 1)
         for j in range(J):

from contextlib import ExitStack

import concourse.mybir as mybir
from concourse.masks import make_identity

L, R, F = 4, 1024, 512
FLOPS = 2 * 2 * L * R * F * F

F32 = mybir.dt.float32
BF16 = mybir.dt.bfloat16
I32 = mybir.dt.int32
U32 = mybir.dt.uint32
U8 = mybir.dt.uint8
FP8X4 = mybir.dt.float8_e4m3fn_x4
FP4X4 = mybir.dt.float4_e2m1fn_x4
ALU = mybir.AluOpType
ACT = mybir.ActivationFunctionType

P = 128
PACK = 4
T = 256
J = T // P
CHUNKS = L * R // T
PER_LAYER = R // T
LATE = 64
ON_GPSIMD = CHUNKS - 2
X_ON_SCALAR = [c for c in range(CHUNKS - 2) if c % 5 in (2, 4)]


def tile_layered_coupled_wave_operator_k7_kernel(
    tc, u, kx, einv_words, einv_scales, eps_words, eps_scales, source, hscale, out_0, out_1, out_2
):
    nc = tc.nc
    u_rows = u.rearrange("l r f -> (l r) f")
    src_rows = source.rearrange("l r f -> (l r) f")
    y_rows = out_0.rearrange("l r f -> (l r) f")
    words_out = out_1[0].rearrange("p m t -> p (m t)").bitcast(I32)
    scales_out = out_2[0].bitcast(I32)

    def chunk_rows(rows, c):
        return rows[c * T : (c + 1) * T, :].rearrange("(p j) f -> p j f", j=J)

    with ExitStack() as ctx:
        keep = ctx.enter_context(tc.tile_pool(name="keep", bufs=1))
        work = ctx.enter_context(tc.tile_pool(name="work", bufs=3))
        psum = ctx.enter_context(tc.psum_pool(name="psum", bufs=1))
        ctx.enter_context(tc.manual_schedule())

        ident = keep.tile([P, P], F32, name="ident")
        kx_bf = keep.tile([P, PACK], BF16, name="kx_bf")
        kx_f32 = keep.tile([P, PACK], F32, name="kx_f32")
        a_raw = keep.tile([P, L, 2 * F], U8, name="a_raw", align_bytes=64)
        a_raw_scales = keep.tile([P, L, F], U8, name="a_raw_scales", align_bytes=64)
        a_words = keep.tile([P, L, 2 * F], U8, name="a_words", align_bytes=64)
        a_scales = keep.tile([P, L, F], U8, name="a_scales", align_bytes=64)
        e_words = keep.tile([P, L, 2 * F], U8, name="e_words", align_bytes=64)
        e_scales = keep.tile([P, L, F], U8, name="e_scales", align_bytes=64)
        h_rep = keep.tile([P, L, F], BF16, name="h_rep")
        y_codes = keep.tile([P, L * R], U32, name="y_codes", align_bytes=64)
        y_scales = keep.tile([P, L * R], U8, name="y_scales", align_bytes=64)
        u_sb = [keep.tile([P, J, F], BF16, name="u_%d" % c) for c in range(CHUNKS)]
        src_sb = [keep.tile([P, J, F], BF16, name="src_%d" % c) for c in range(CHUNKS)]

        def load_words(dst, words, l0, l1):
            nc.sync.dma_start(
                out=dst[:, l0:l1, :].bitcast(I32), in_=words[l0:l1].rearrange("l p n -> p l n").bitcast(I32)
            )

        def load_scales(dst, scales):
            for q in range(4):
                nc.scalar.dma_start(
                    out=dst[32 * q : 32 * q + 4, :, :].bitcast(I32),
                    in_=scales[:, 4 * q : 4 * q + 4, :].rearrange("l r n -> r l n").bitcast(I32),
                )

        def load_h(l):
            nc.sync.dma_start(out=h_rep[:, l, :], in_=hscale[l].partition_broadcast(P))

        nc.vector.memset(a_raw_scales[:].bitcast(I32), 0)
        nc.vector.memset(e_scales[:].bitcast(I32), 0)
        make_identity(nc, ident[:])
        nc.sync.dma_start(out=u_sb[0][:], in_=chunk_rows(u_rows, 0))
        nc.scalar.dma_start(out=kx_bf[:], in_=kx.rearrange("(p t) -> p t", t=PACK))
        load_words(a_raw, einv_words, 0, 1)
        load_scales(a_raw_scales, einv_scales)
        nc.sync.dma_start(out=u_sb[1][:], in_=chunk_rows(u_rows, 1))
        load_words(a_raw, einv_words, 1, L)
        load_words(e_words, eps_words, 0, 1)
        load_scales(e_scales, eps_scales)
        nc.scalar.activation(out=kx_f32[:], in_=kx_bf[:], func=ACT.Copy)
        for c in range(CHUNKS):
            if c + 2 < CHUNKS:
                nc.sync.dma_start(out=u_sb[c + 2][:], in_=chunk_rows(u_rows, c + 2))
            nc.sync.dma_start(out=src_sb[c][:], in_=chunk_rows(src_rows, c))
            if c % PER_LAYER == 0:
                load_h(c // PER_LAYER)
            if c == 1:
                load_words(e_words, eps_words, 1, L)

        uT, x_bf, xq, xs, hp, hk, z_bf, zq, zs, vp, w, y, y_bf, yT, y_il = ({} for n in range(15))
        x_rows = {}

        def permute_words(l):
            nc.vector.tensor_copy(
                out=a_words[:, l, :].rearrange("p (t m b) -> p t m b", t=PACK, b=2),
                in_=a_raw[:, l, :].rearrange("p (m t b) -> p t m b", t=PACK, b=2),
            )

        def permute_scales(l):
            nc.vector.tensor_copy(
                out=a_scales[:, l, :].rearrange("p (t m) -> p t m", t=PACK),
                in_=a_raw_scales[:, l, :].rearrange("p (m t) -> p t m", t=PACK),
            )

        def transpose_words(dst, rows):
            for j in range(J):
                pairs = rows[:, j, :].bitcast(F32)
                for s in range(2):
                    nc.tensor.transpose(dst[:, s, j * P : (j + 1) * P], pairs[:, s : F // 2 : 2], ident[:])

        def transpose_u(c):
            uT[c] = psum.tile([P, 2, T], F32, name="uT", bufs=3)
            transpose_words(uT[c], u_sb[c])

        def u_view(c):
            return uT[c][:].bitcast(BF16).rearrange("p s (n e) -> p n s e", e=2)

        def make_x(c):
            x_bf[c] = work.tile([P, T * PACK], BF16, name="x_bf", align_bytes=64)
            nc.vector.tensor_tensor(
                out=x_bf[c][:].rearrange("p (n s e) -> p n s e", s=2, e=2),
                in0=kx_bf[:].rearrange("p (s e) -> p s e", e=2).unsqueeze(1).to_broadcast([P, T, 2, 2]),
                in1=u_view(c),
                op=ALU.mult,
            )

        def scale_u(c):
            x_rows[c] = work.tile([P, PACK, T], BF16, name="x_rows", bufs=2)
            for t in range(PACK):
                nc.scalar.activation(
                    out=x_rows[c][:, t, :],
                    in_=uT[c][:, t // 2, :].bitcast(BF16)[:, t % 2 : 2 * T : 2],
                    func=ACT.Copy,
                    scale=kx_f32[:, t : t + 1],
                )

        def interleave_x(c):
            x_bf[c] = work.tile([P, T * PACK], BF16, name="x_bf", align_bytes=64)
            nc.scalar.copy(
                out=x_bf[c][:].rearrange("p (n t) -> p n t", t=PACK), in_=x_rows[c][:].rearrange("p t n -> p n t")
            )

        def quantize_x(c):
            xq[c] = work.tile([P, T], U32, name="xq", align_bytes=64)
            xs[c] = work.tile([P, T], U8, name="xs", align_bytes=64)
            nc.vector.quantize_mx(out=xq[c][:].bitcast(FP8X4), scales=xs[c][:], in_=x_bf[c][:])

        def matmul_h(c, s):
            l = c // PER_LAYER
            hp[c, s] = psum.tile([P, 2, T], F32, name="hp%d" % s)
            for e in range(2):
                t = 2 * s + e
                nc.tensor.matmul_mx(
                    out=hp[c, s][:, e, :],
                    lhsT=a_words[:, l, 2 * P * t : 2 * P * (t + 1)].bitcast(FP4X4),
                    lhsT_scale=a_scales[:, l, P * t : P * (t + 1)],
                    rhs=xq[c][:].bitcast(FP8X4),
                    rhs_scale=xs[c][:],
                    start=True,
                    stop=True,
                )

        def scale_h(c):
            hk[c] = work.tile([P, PACK, T], F32, name="hk")
            for t in range(PACK):
                nc.scalar.activation(
                    out=hk[c][:, t, :], in_=hp[c, t // 2][:, t % 2, :], func=ACT.Copy, scale=kx_f32[:, t : t + 1]
                )

        def make_z(c):
            z_bf[c] = work.tile([P, T * PACK], BF16, name="z_bf", align_bytes=64)
            nc.vector.tensor_tensor(
                out=z_bf[c][:].rearrange("p (n s e) -> p n s e", s=2, e=2),
                in0=hk[c][:].rearrange("p (s e) n -> p n s e", e=2),
                in1=u_view(c),
                op=ALU.subtract,
            )

        def quantize_z(c):
            zq[c] = work.tile([P, T], U32, name="zq", align_bytes=64)
            zs[c] = work.tile([P, T], U8, name="zs", align_bytes=64)
            nc.vector.quantize_mx(out=zq[c][:].bitcast(FP8X4), scales=zs[c][:], in_=z_bf[c][:])

        def matmul_v(c, j):
            vp[c, j] = psum.tile([P, F], F32, name="vp%d" % j)
            product_v(vp[c, j][:], c, j)

        def product_v(dst, c, j):
            l = c // PER_LAYER
            nc.tensor.matmul_mx(
                out=dst,
                lhsT=zq[c][:, j * P : (j + 1) * P].bitcast(FP8X4),
                lhsT_scale=zs[c][:, j * P : (j + 1) * P],
                rhs=e_words[:, l, :].bitcast(FP4X4),
                rhs_scale=e_scales[:, l, :],
                start=True,
                stop=True,
            )

        def add_source(c, j, f0, f1):
            nc.vector.tensor_tensor(
                out=w[c][:, j, f0:f1], in0=src_sb[c][:, j, f0:f1], in1=vp[c, j][:, f0:f1], op=ALU.add
            )

        def add_source_early(c):
            w[c] = work.tile([P, J, F], F32, name="w")
            add_source(c, 0, 0, F)
            add_source(c, 1, 0, F - LATE if c < ON_GPSIMD else F)

        def make_y(c):
            l = c // PER_LAYER
            y[c] = work.tile([P, J, F], F32, name="y", bufs=4)
            nc.gpsimd.tensor_tensor(
                out=y[c][:], in0=w[c][:], in1=h_rep[:, l, :].unsqueeze(1).to_broadcast([P, J, F]), op=ALU.mult
            )
            nc.sync.dma_start(out=chunk_rows(y_rows, c), in_=y[c][:])

        def pair_order(rows):
            return rows.rearrange("p j (s m e) -> p j s m e", s=2, e=2)

        def pairs_of(rows):
            return rows.rearrange("p j (m s e) -> p j s m e", s=2, e=2)

        def round_y(c):
            y_bf[c] = work.tile([P, J, F], BF16, name="y_bf")
            nc.scalar.copy(out=pair_order(y_bf[c][:]), in_=pairs_of(y[c][:]))

        def transpose_y(c):
            yT[c] = psum.tile([P, 2, T], F32, name="yT")
            for j in range(J):
                pairs = y_bf[c][:, j, :].bitcast(F32)
                for s in range(2):
                    nc.tensor.transpose(yT[c][:, s, j * P : (j + 1) * P], pairs[:, s * P : (s + 1) * P], ident[:])
            y_il[c] = work.tile([P, T * PACK], BF16, name="y_il", bufs=5, align_bytes=64)
            nc.scalar.copy(
                out=y_il[c][:].bitcast(F32).rearrange("p (n j s) -> p n j s", j=J, s=2),
                in_=yT[c][:].rearrange("p s (j n) -> p n j s", j=J),
            )

        def quantize_y(c):
            cols = slice(c * T, (c + 1) * T)
            nc.vector.quantize_mx(out=y_codes[:, cols].bitcast(FP8X4), scales=y_scales[:, cols], in_=y_il[c][:])
            nc.sync.dma_start(out=words_out[:, cols], in_=y_codes[:, cols].bitcast(I32))
            if c in (11, 15):
                c0 = 0 if c == 11 else 12
                for q in range(4):
                    nc.sync.dma_start(
                        out=scales_out[4 * q : 4 * q + 4, c0 * T // 4 : (c + 1) * T // 4],
                        in_=y_scales[32 * q : 32 * q + 4, c0 * T : (c + 1) * T].bitcast(I32),
                    )

        def finish_half(c, j):
            l = c // PER_LAYER
            nc.vector.tensor_tensor(out=y[c][:, j, :], in0=w[c][:, j, :], in1=h_rep[:, l, :], op=ALU.mult)
            nc.sync.dma_start(out=chunk_rows(y_rows, c)[:, j, :], in_=y[c][:, j, :])

        def live(c):
            return 0 <= c < CHUNKS

        transpose_u(0)
        transpose_u(1)
        permute_words(0)
        make_x(0)
        permute_scales(0)
        for i in range(-1, CHUNKS):
            if live(i - 1):
                quantize_z(i - 1)
            if live(i + 1):
                quantize_x(i + 1)
            x_on_vector = live(i + 2) and i + 2 not in X_ON_SCALAR
            if live(i - 5) and x_on_vector:
                quantize_y(i - 5)
            if 0 <= i - 2 < ON_GPSIMD:
                add_source(i - 2, 1, F - LATE, F)
            if live(i - 5) and not x_on_vector:
                quantize_y(i - 5)
            if 0 <= i - 2 < ON_GPSIMD:
                make_y(i - 2)
            if live(i - 3):
                round_y(i - 3)
            if i + 2 in X_ON_SCALAR:
                interleave_x(i + 2)
            if live(i - 1):
                matmul_v(i - 1, 0)
            if live(i + 1):
                matmul_h(i + 1, 0)
                matmul_h(i + 1, 1)
                scale_h(i + 1)
            if live(i - 1):
                matmul_v(i - 1, 1)
            if x_on_vector:
                make_x(i + 2)
            if i == -1:
                permute_words(1)
                permute_scales(1)
                permute_words(2)
            if live(i):
                make_z(i)
            if i == 0:
                permute_scales(2)
                permute_words(3)
                permute_scales(3)
            if live(i - 1):
                add_source_early(i - 1)
            if live(i - 3):
                transpose_y(i - 3)
            if live(i + 3):
                transpose_u(i + 3)
            if i + 3 in X_ON_SCALAR:
                scale_u(i + 3)

        a, b = CHUNKS - 2, CHUNKS - 1
        round_y(a - 1)
        for c in (a, b):
            y[c] = work.tile([P, J, F], F32, name="y", bufs=4)
            y_bf[c] = work.tile([P, J, F], BF16, name="y_bf")
        w[b] = work.tile([P, J, F], F32, name="w")
        quantize_z(b)
        quantize_y(a - 3)
        matmul_v(b, 0)
        matmul_v(b, 1)
        for j in range(J):
            finish_half(a, j)
            nc.scalar.copy(out=pair_order(y_bf[a][:, j : j + 1, :]), in_=pairs_of(y[a][:, j : j + 1, :]))
        transpose_y(a - 1)
        transpose_y(a)
        for j in range(J):
            add_source(b, j, 0, F)
        for j in range(J):
            finish_half(b, j)
        for j in range(J):
            nc.vector.tensor_copy(out=pair_order(y_bf[b][:, j : j + 1, :]), in_=pairs_of(y[b][:, j : j + 1, :]))
        quantize_y(a - 2)
        quantize_y(a - 1)
        transpose_y(b)
        quantize_y(a)
        quantize_y(b)
